import numpy as np
CORES = [0,1,2,3,4,5,6,7,8,9,10,11,12,13,14,15,16,17,18,19,20,21,22,23,24,25,26,27,28,29,30,31,32,33,34,35,36,37,38,39,40,41,42,43,44,45,46,47,48,49,50,51,52,53,54,55,56,57,58,59,60,61,62,63,64,65,66,67,68,69,70,71,72,73,74,75,76,77,78,79,80,81,82,83,84,85,86,87,88,89,90,91,92,93,94,95,96,97,98,99,100,101,102,103,104,105,106,107,108,109,110,111,112,113,114,115,116,117,118,119,120,121,122,123,124,125,126,127,128,129,130,131,132,133,134,135,136,137,138,139,140,141,142,143,144,145,146,147,148,149,150,151,152,153,154,155,156,157,158,159,160,161,162,163,164,165,166,167,168,169,170,171,172,173,174,175,176,177,178,179,180,181,182,183,184,185,186,187,188,189,190,191,192,193,194,195,196,197,198,199,200,201,202,203,204,205,206,207,208,209,210,211,212,213,214,215,216,217,218,219,220,221,222,223,224,225,226,227,228,229,230,231,232,233,234,235,236,237,238,239,240,241,242,243,244,245,246,247,248,249,250,251,252,253,254,255]
N = 256
def setup_inputs(rng):
    return {"x": rng.standard_normal((N, 128, 16), dtype=np.float32)}
def reference(x):
    g = np.concatenate(list(x), axis=1)
    return {"y": np.broadcast_to(g, (N,) + g.shape)}

import concourse.bass as bass

BLK = 16
CHIPBLK = 8 * BLK
RANGE = 4 * CHIPBLK

SCRATCH = {
    "land": ("sbuf", [128, 256 * BLK], "float32"),
    "xs": ("sbuf", [128, BLK], "float32"),
}
SEMAPHORES = ["loaded", "stored", "sent", "hop1", "hop2", "hop3", "hop4"]


def owner_of(chip, blk):
    return 4 * (blk // 16) + ((blk % 16) // 4 - chip // 4) % 4


def collector_of(chip, blk):
    o = owner_of(chip, blk)
    return o if o % 4 >= 2 else o + 2


def rank_program(g, core, T, topo):
    host, chip, k = topo.host(core), topo.chip(core), core % 8
    pos = k % 4
    land, sem = T.land, T.sem
    sent = 0

    def world(h, c, i):
        return 128 * h + 8 * c + i

    def here(i):
        return world(host, chip, i)

    def cols(blk, n=1):
        return land[:, CHIPBLK * blk:CHIPBLK * (blk + n)]

    def transfer(src, out, dests, mask, remote_sem):
        ids = []
        for d in dests:
            rid, pid = topo.addr(d, core)
            ids.append(bass.DstId(rid=rid, pnc=pid))
        return bass.RemoteDMATransfer(dst_ids=ids, dma_engine_mask=mask, remote_sem=remote_sem,
                                      srcs=[src], dsts=[out for d in dests])

    rank = T.rank_of(core)
    mine = land[:, BLK * rank:BLK * (rank + 1)]
    gatherer = 4 * host
    staged = mine if k == gatherer else T.xs[:]
    g.dma_start(staged, T.x[:]).then_inc(sem.loaded, 16)
    g.wait_ge(sem.loaded, 16)

    dests = [world(1 - host, chip, gatherer)]
    if k != gatherer:
        dests.append(here(gatherer))
    g.remote_dma_fused([transfer(staged, mine, dests, 0x00FF, sem.hop1)], local_sem=sem.sent)
    sent += 8

    if pos == 0:
        blk = 16 * (k // 4) + chip
        g.wait_ge(sem.hop1, 8 * (7 if k == gatherer else 8))
        dests = [world(host, c, collector_of(c, blk)) for c in range(chip % 2, 16, 2) if c != chip]
        dests.append(here(k + 2))
        g.remote_dma_fused([transfer(cols(blk), cols(blk), dests, 0x00FF, sem.hop2)], local_sem=sem.sent)
        sent += 8

    first = 4 * (4 * (k // 4) + (pos + chip // 4) % 4)
    same = [first + chip % 2, first + 2 + chip % 2]
    other = [first + 1 - chip % 2, first + 3 - chip % 2]

    if pos >= 2:
        g.wait_ge(sem.hop2, 8 * 4)
        pfirst = 4 * (4 * (k // 4) + (pos - 2 + chip // 4) % 4)
        calls = []
        for n, blk in enumerate(same + [pfirst + chip % 2, pfirst + 2 + chip % 2]):
            o = owner_of(chip, blk)
            dests = [world(host, chip ^ 1, o)]
            if o != k and blk % 16 != chip:
                dests.append(here(o))
            calls.append(transfer(cols(blk), cols(blk), dests, 0x03 << (2 * n), sem.hop3))
        g.remote_dma_fused(calls, local_sem=sem.sent)
        sent += 8

    g.wait_ge(sem.hop3, 2 * (2 if pos >= 2 else 3 if pos == 0 else 4))
    dests = [here(i) for i in range(8) if i != k and (pos >= 2 or i != k + 2)]
    g.remote_dma_fused([transfer(cols(first, 4), cols(first, 4), dests, 0xFFFF, sem.hop4)], local_sem=sem.sent)
    sent += 16
    if pos < 2:
        g.remote_dma_fused([transfer(cols(b), cols(b), [here(k + 2)], 0x00FF << (8 * n), sem.hop4)
                            for n, b in enumerate(other)], local_sem=sem.sent)
        sent += 16

    g.wait_ge(sem.hop4, 16 * 7)
    g.wait_ge(sem.sent, sent)
    g.dma_start(T.y[:], land[:]).then_inc(sem.stored, 16)
    g.wait_ge(sem.stored, 16)
